import numpy as np
import ml_dtypes


def mxq(x, axis, fmt="e4m3"):
    dtype, down = {"e4m3": (ml_dtypes.float8_e4m3fn, 7), "e5m2": (ml_dtypes.float8_e5m2, 14)}[fmt]
    v = np.moveaxis(np.asarray(x, np.float32).astype(ml_dtypes.bfloat16).astype(np.float64), axis, -1)
    blocks = v.reshape(v.shape[:-1] + (-1, 32))
    amax = np.abs(blocks).max(-1, keepdims=True)
    byte = np.maximum(np.where(amax > 0, np.frexp(amax)[1] - 1 + 127, 0) - down, 1)
    scale = np.exp2(byte - 127.0)
    codes = (blocks / scale).astype(np.float32).astype(dtype).astype(np.float64)
    return np.moveaxis((codes * scale).reshape(v.shape), -1, axis)


WIDE = False


def mx_kscale(k):
    if not WIDE:
        return np.ones(k)
    levels = np.array([10, -10, 5, -5, 0])
    if k % 512:
        return np.exp2(np.random.permutation(np.resize(levels, k // 32))).repeat(32)
    a = np.empty((k // 512, 16))
    for p in range(k // 512):
        a[p, :8] = np.random.permutation(np.resize(levels, 8))
        for g in range(8):
            far = levels[np.abs(levels - a[p, g]) >= 10]
            a[p, g + 8] = far[np.random.randint(len(far))]
    return np.exp2(a.ravel()).repeat(32)


def f64(x):
    return np.asarray(x).astype(np.float64)


def striped(idx):
    return np.tile(np.asarray(idx).reshape(-1, 16).T, (8, 1)).astype(np.uint16)


def unstriped(offs):
    return offs[:16].T.reshape(-1).astype(np.int64)


E2M1 = np.array([0.0, 0.5, 1.0, 1.5, 2.0, 3.0, 4.0, 6.0, -0.0, -0.5, -1.0, -1.5, -2.0, -3.0, -4.0, -6.0])


def pack_weight(w, fmt):
    k, n = w.shape
    w = f64(np.asarray(w, np.float32).astype(ml_dtypes.bfloat16)).reshape(k // 32, 32, n)
    amax = np.abs(w).max(1)
    if fmt == "e4m3":
        byte = np.frexp(amax)[1] - 1 + 127 - 7
    else:
        mant, ex = np.frexp(amax / 6.0)
        byte = np.where(mant > 0.5, ex, ex - 1) + 127
    byte = np.clip(np.where(amax > 0, byte, 1), 1, 254)
    scaled = (w * np.exp2(127.0 - byte)[:, None, :]).reshape(k, n).astype(np.float32)
    by_word = np.ascontiguousarray(scaled.reshape(k // 512, 128, 4, n).transpose(0, 1, 3, 2))
    if fmt == "e4m3":
        words = by_word.astype(ml_dtypes.float8_e4m3fn).view(np.uint8)
    else:
        c = by_word.astype(ml_dtypes.float4_e2m1fn).view(np.uint8) & 0xF
        words = (c[..., 0::2] | (c[..., 1::2] << 4)).reshape(k // 512, 128, 2 * n)
    return np.ascontiguousarray(words), np.ascontiguousarray(byte.astype(np.uint8).reshape(k // 512, 16, n))


def unpack_weight(words, scales, fmt):
    g, _, n = scales.shape
    words = np.ascontiguousarray(words).reshape(g, 128, n, -1)
    if fmt == "e4m3":
        vals = words.view(ml_dtypes.float8_e4m3fn).astype(np.float64)
    else:
        nib = np.empty((g, 128, n, 4), np.uint8)
        nib[..., 0::2] = words & 0xF
        nib[..., 1::2] = words >> 4
        vals = E2M1[nib]
    vals = vals * np.repeat(np.exp2(scales.astype(np.float64) - 127.0), 8, axis=1)[..., None]
    return vals.transpose(0, 1, 3, 2).reshape(g * 512, n)


def sigmoid(v):
    return 1.0 / (1.0 + np.exp(-v))


B, N, T, D, NQ = 1, 512, 2048, 512, 256


def setup_inputs():
    n = np.random.standard_normal
    idx = np.random.permutation(T)[:B * N]
    s = mx_kscale(D)[:, None]
    kp = pack_weight(n((D, T)) / s, "e4m3")
    return {
        "qT": (n((B, D, NQ)) * s * (1.00 / np.sqrt(D))).astype(np.float32),
        "k_words": kp[0],
        "k_scales": kp[1],
        "kb": np.tile(n(2048) - 1, (128, 1)).astype(np.float32),
        "bd": np.tile(np.random.uniform(0.1, 2.0, 2048), (128, 1)).astype(np.float32),
        "offs": striped(idx),
    }


def reference(qT, k_words, k_scales, kb, bd, offs):
    idx = unstriped(offs)
    pick = lambda x, which: x[:, which].reshape(x.shape[0], B, -1).transpose(1, 0, 2)
    k = unpack_weight(k_words, k_scales, "e4m3")
    kg = pick(k, idx)
    qq = mxq(f64(qT), 1, "e4m3")
    a = qq.transpose(0, 2, 1) @ kg
    y = sigmoid(a + pick(f64(kb), idx)[:, :1, :]) * pick(f64(bd), idx)[:, :1, :]
    return y

@@ -1,0 +1,121 @@
+from contextlib import ExitStack
+
+import concourse.mybir as mybir
+from concourse.masks import make_identity
+
+F32 = mybir.dt.float32
+BF16 = mybir.dt.bfloat16
+I32 = mybir.dt.int32
+U32 = mybir.dt.uint32
+U16 = mybir.dt.uint16
+U8 = mybir.dt.uint8
+FP8X4 = mybir.dt.float8_e4m3fn_x4
+ACT = mybir.ActivationFunctionType
+ALU = mybir.AluOpType
+
+P = 128
+PACK = 4
+T = 2048
+N = 512
+NQ = 256
+D = 512
+SLOT_TILES = N // P
+Q_TILES = NQ // P
+HALF = N // 2
+
+FLOPS = 2 * D * NQ * N
+
+
+def tile_attend_link_bid_topk_kernel(tc, qT, k_words, k_scales, kb, bd, offs, out):
+    nc = tc.nc
+    with ExitStack() as ctx:
+        keep = ctx.enter_context(tc.tile_pool(name="keep", bufs=1))
+        score_psum = ctx.enter_context(tc.psum_pool(name="score_psum", bufs=SLOT_TILES))
+        turn_psum = ctx.enter_context(tc.psum_pool(name="turn_psum", bufs=SLOT_TILES))
+
+        offsets = keep.tile([P, N // 16], U16, name="offsets")
+        nc.sync.dma_start(offsets[:], offs)
+
+        scale_win = keep.tile([P, T], U8, name="scale_win", align_bytes=64)
+        nc.vector.memset(scale_win[:].bitcast(I32), 0)
+        kb_win = keep.tile([P, T], F32, name="kb_win")
+        nc.sync.dma_start(out=kb_win[P - 1 : P, :], in_=kb[0:1, :])
+        nc.vector.memset(kb_win[0 : P - 1, :].bitcast(I32), 0)
+
+        scale_rows = k_scales[0].bitcast(I32)
+        for r in range(4):
+            nc.scalar.dma_start(out=scale_win[:].bitcast(I32)[r:P:32, :], in_=scale_rows[r:16:4, :])
+
+        q_raw = keep.tile([P, PACK, NQ], F32, name="q_raw")
+        nc.sync.dma_start(out=q_raw[:], in_=qT[0].rearrange("(p j) w -> p j w", j=PACK))
+        word_win = keep.tile([P, T], I32, name="word_win")
+        nc.sync.dma_start(out=word_win[:], in_=k_words[0].rearrange("p n t -> p (n t)").bitcast(I32))
+        bd_win = keep.tile([P, T], F32, name="bd_win")
+        bd_cols = keep.tile([P, T // P], F32, name="bd_cols")
+        nc.gpsimd.dma_start(out=bd_cols[:], in_=bd[0].rearrange("(p j) -> p j", p=P))
+
+        ident = keep.tile([P, P], F32, name="ident")
+        make_identity(nc, ident[:])
+        warm = keep.tile([P, 1], F32, name="warm")
+        nc.scalar.activation(warm[:], ident[:, 0:1], ACT.Sigmoid)
+
+        kb_g = keep.tile([P, N], F32, name="kb_g")
+        nc.vector.tensor_copy(kb_g[:], kb_win[:].indirect(offsets[:]))
+        scale_g = keep.tile([P, N], U8, name="scale_g", align_bytes=64)
+        nc.vector.tensor_copy(scale_g[:], scale_win[:].indirect(offsets[:]))
+
+        q_grp = keep.tile([P, NQ, PACK], BF16, name="q_grp", align_bytes=64)
+        nc.scalar.copy(
+            out=q_grp[:].rearrange("p (c i) t -> p c t i", i=4),
+            in_=q_raw[:].rearrange("p t (c i) -> p c t i", i=4),
+        )
+        q_codes = keep.tile([P, NQ], U32, name="q_codes", align_bytes=64)
+        q_scales = keep.tile([P, NQ], U8, name="q_scales", align_bytes=64)
+        nc.vector.quantize_mx(out=q_codes[:].bitcast(FP8X4), scales=q_scales[:], in_=q_grp[:].rearrange("p w j -> p (w j)"))
+
+        kb_turned = turn_psum.tile([P, SLOT_TILES, P], F32, name="kb_turned", tag="turn")
+        for j in range(SLOT_TILES):
+            nc.tensor.transpose(kb_turned[:, j, :], kb_g[:, j * P : (j + 1) * P], ident[:])
+        kb_col = keep.tile([P, SLOT_TILES], F32, name="kb_col")
+        nc.scalar.copy(out=kb_col[:], in_=kb_turned[:, :, P - 1])
+
+        bd_by_run = bd_win[:].rearrange("r (p b i) -> r p b i", p=P, i=4)
+        for b in range(T // P // 4):
+            spread = turn_psum.tile([P, 4, P], F32, name="spread", tag="turn")
+            for i in range(4):
+                c = 4 * b + i
+                nc.tensor.transpose(spread[:, i, :], bd_cols[:, c : c + 1].to_broadcast([P, P]), ident[:])
+            nc.scalar.copy(out=bd_by_run[:, :, b, :], in_=spread[:].rearrange("r i p -> r p i"))
+
+        word_g = [keep.tile([P, HALF], U32, name="word_g%d" % h, align_bytes=64) for h in range(2)]
+        for h in range(2):
+            nc.vector.tensor_copy(word_g[h][:], word_win[:].bitcast(U32).indirect(offsets[:, h * 16 : (h + 1) * 16]))
+        bd_g = keep.tile([P, N], F32, name="bd_g")
+        nc.vector.tensor_copy(bd_g[:], bd_win[:].indirect(offsets[:]))
+
+        probs = []
+        for j in range(SLOT_TILES):
+            score = score_psum.tile([P, NQ], F32, name="score", tag="score")
+            nc.tensor.matmul_mx(
+                out=score[:],
+                lhsT=word_g[j // 2][:, (j % 2) * P : (j % 2 + 1) * P].bitcast(FP8X4),
+                lhsT_scale=scale_g[:, j * P : (j + 1) * P],
+                rhs=q_codes[:].bitcast(FP8X4),
+                rhs_scale=q_scales[:],
+                start=True,
+                stop=True,
+            )
+            prob = keep.tile([P, NQ], F32, name="prob%d" % j)
+            nc.scalar.activation(prob[:], score[:], ACT.Sigmoid, bias=kb_col[:, j : j + 1])
+            probs.append(prob)
+
+        out_v = out[0].rearrange("(u p) n -> p u n", p=P)
+        for j in range(SLOT_TILES):
+            turned = turn_psum.tile([P, Q_TILES, P], F32, name="turned", tag="turn")
+            for u in range(Q_TILES):
+                nc.tensor.transpose(turned[:, u, :], probs[j][:, u * P : (u + 1) * P], ident[:])
+            res = keep.tile([P, Q_TILES, P], F32, name="res%d" % j)
+            nc.vector.tensor_tensor(
+                res[:], turned[:], bd_g[:, j * P : (j + 1) * P].unsqueeze(1).to_broadcast([P, Q_TILES, P]), ALU.mult
+            )
+            nc.sync.dma_start(out=out_v[:, :, j * P : (j + 1) * P], in_=res[:])

@@ -22,6 +22,8 @@ D = 512
 SLOT_TILES = N // P
 Q_TILES = NQ // P
 HALF = N // 2
+SPREAD_BANKS = 4
+LOADED = T - 4 * P * SPREAD_BANKS
 
 FLOPS = 2 * D * NQ * N
 
@@ -36,40 +38,51 @@ def tile_attend_link_bid_topk_kernel(tc, qT, k_words, k_scales, kb, bd, offs, ou
         offsets = keep.tile([P, N // 16], U16, name="offsets")
         nc.sync.dma_start(offsets[:], offs)
 
-        scale_win = keep.tile([P, T], U8, name="scale_win", align_bytes=64)
+        bd_cols = keep.tile([P, 4 * SPREAD_BANKS], F32, name="bd_cols")
+        nc.sync.dma_start(out=bd_cols[:], in_=bd[0, LOADED:T].rearrange("(p j) -> p j", p=P))
+
+        scale_win = keep.tile([P, T], U8, name="scale_win", tag="scales_then_q_codes", align_bytes=64)
         nc.vector.memset(scale_win[:].bitcast(I32), 0)
-        kb_win = keep.tile([P, T], F32, name="kb_win")
+        warm_in = keep.tile([P, 1], F32, name="warm_in")
+        nc.gpsimd.memset(warm_in[:], 0.0)
+        kb_win = keep.tile([P, T], F32, name="kb_win", tag="bias_then_scales", align_bytes=64)
         nc.sync.dma_start(out=kb_win[P - 1 : P, :], in_=kb[0:1, :])
         nc.vector.memset(kb_win[0 : P - 1, :].bitcast(I32), 0)
 
         scale_rows = k_scales[0].bitcast(I32)
         for r in range(4):
-            nc.scalar.dma_start(out=scale_win[:].bitcast(I32)[r:P:32, :], in_=scale_rows[r:16:4, :])
+            nc.sync.dma_start(out=scale_win[:].bitcast(I32)[r:P:32, :], in_=scale_rows[r:16:4, :])
 
         q_raw = keep.tile([P, PACK, NQ], F32, name="q_raw")
-        nc.sync.dma_start(out=q_raw[:], in_=qT[0].rearrange("(p j) w -> p j w", j=PACK))
-        word_win = keep.tile([P, T], I32, name="word_win")
-        nc.sync.dma_start(out=word_win[:], in_=k_words[0].rearrange("p n t -> p (n t)").bitcast(I32))
-        bd_win = keep.tile([P, T], F32, name="bd_win")
-        bd_cols = keep.tile([P, T // P], F32, name="bd_cols")
-        nc.gpsimd.dma_start(out=bd_cols[:], in_=bd[0].rearrange("(p j) -> p j", p=P))
+        nc.scalar.dma_start(out=q_raw[:], in_=qT[0].rearrange("(p j) w -> p j w", j=PACK))
+        word_win = keep.tile([P, T], I32, name="word_win", tag="words_then_bids")
+        nc.scalar.dma_start(out=word_win[:], in_=k_words[0].rearrange("p n t -> p (n t)").bitcast(I32))
 
         ident = keep.tile([P, P], F32, name="ident")
         make_identity(nc, ident[:])
         warm = keep.tile([P, 1], F32, name="warm")
-        nc.scalar.activation(warm[:], ident[:, 0:1], ACT.Sigmoid)
+        nc.scalar.activation(warm[:], warm_in[:], ACT.Sigmoid)
+
+        bd_win = keep.tile([P, T], F32, name="bd_win")
+        bd_by_run = bd_win[:, LOADED:T].rearrange("r (p b i) -> r p b i", p=P, i=4)
+        for b in range(SPREAD_BANKS):
+            spread = turn_psum.tile([P, 4, P], F32, name="spread", tag="turn")
+            for i in range(4):
+                c = 4 * b + i
+                nc.tensor.transpose(spread[:, i, :], bd_cols[:, c : c + 1].to_broadcast([P, P]), ident[:])
+            nc.scalar.copy(out=bd_by_run[:, :, b, :], in_=spread[:].rearrange("r i p -> r p i"))
 
         kb_g = keep.tile([P, N], F32, name="kb_g")
         nc.vector.tensor_copy(kb_g[:], kb_win[:].indirect(offsets[:]))
-        scale_g = keep.tile([P, N], U8, name="scale_g", align_bytes=64)
+        scale_g = keep.tile([P, N], U8, name="scale_g", tag="bias_then_scales", align_bytes=64)
         nc.vector.tensor_copy(scale_g[:], scale_win[:].indirect(offsets[:]))
 
-        q_grp = keep.tile([P, NQ, PACK], BF16, name="q_grp", align_bytes=64)
+        q_grp = keep.tile([P, NQ, PACK], BF16, name="q_grp", tag="q_then_words", align_bytes=64)
         nc.scalar.copy(
             out=q_grp[:].rearrange("p (c i) t -> p c t i", i=4),
             in_=q_raw[:].rearrange("p t (c i) -> p c t i", i=4),
         )
-        q_codes = keep.tile([P, NQ], U32, name="q_codes", align_bytes=64)
+        q_codes = keep.tile([P, NQ], U32, name="q_codes", tag="scales_then_q_codes", align_bytes=64)
         q_scales = keep.tile([P, NQ], U8, name="q_scales", align_bytes=64)
         nc.vector.quantize_mx(out=q_codes[:].bitcast(FP8X4), scales=q_scales[:], in_=q_grp[:].rearrange("p w j -> p (w j)"))
 
@@ -79,18 +92,10 @@ def tile_attend_link_bid_topk_kernel(tc, qT, k_words, k_scales, kb, bd, offs, ou
         kb_col = keep.tile([P, SLOT_TILES], F32, name="kb_col")
         nc.scalar.copy(out=kb_col[:], in_=kb_turned[:, :, P - 1])
 
-        bd_by_run = bd_win[:].rearrange("r (p b i) -> r p b i", p=P, i=4)
-        for b in range(T // P // 4):
-            spread = turn_psum.tile([P, 4, P], F32, name="spread", tag="turn")
-            for i in range(4):
-                c = 4 * b + i
-                nc.tensor.transpose(spread[:, i, :], bd_cols[:, c : c + 1].to_broadcast([P, P]), ident[:])
-            nc.scalar.copy(out=bd_by_run[:, :, b, :], in_=spread[:].rearrange("r i p -> r p i"))
-
-        word_g = [keep.tile([P, HALF], U32, name="word_g%d" % h, align_bytes=64) for h in range(2)]
+        word_g = keep.tile([P, N], U32, name="word_g", tag="q_then_words", align_bytes=64)
         for h in range(2):
-            nc.vector.tensor_copy(word_g[h][:], word_win[:].bitcast(U32).indirect(offsets[:, h * 16 : (h + 1) * 16]))
-        bd_g = keep.tile([P, N], F32, name="bd_g")
+            nc.vector.tensor_copy(word_g[:, h * HALF : (h + 1) * HALF], word_win[:].bitcast(U32).indirect(offsets[:, h * 16 : (h + 1) * 16]))
+        bd_g = keep.tile([P, N], F32, name="bd_g", tag="words_then_bids")
         nc.vector.tensor_copy(bd_g[:], bd_win[:].indirect(offsets[:]))
 
         probs = []
@@ -98,7 +103,7 @@ def tile_attend_link_bid_topk_kernel(tc, qT, k_words, k_scales, kb, bd, offs, ou
             score = score_psum.tile([P, NQ], F32, name="score", tag="score")
             nc.tensor.matmul_mx(
                 out=score[:],
-                lhsT=word_g[j // 2][:, (j % 2) * P : (j % 2 + 1) * P].bitcast(FP8X4),
+                lhsT=word_g[:, j * P : (j + 1) * P].bitcast(FP8X4),
                 lhsT_scale=scale_g[:, j * P : (j + 1) * P],
                 rhs=q_codes[:].bitcast(FP8X4),
                 rhs_scale=q_scales[:],

@@ -1,7 +1,6 @@
 from contextlib import ExitStack
 
 import concourse.mybir as mybir
-from concourse.masks import make_identity
 
 F32 = mybir.dt.float32
 BF16 = mybir.dt.bfloat16
@@ -22,8 +21,6 @@ D = 512
 SLOT_TILES = N // P
 Q_TILES = NQ // P
 HALF = N // 2
-SPREAD_BANKS = 4
-LOADED = T - 4 * P * SPREAD_BANKS
 
 FLOPS = 2 * D * NQ * N
 
@@ -38,50 +35,45 @@ def tile_attend_link_bid_topk_kernel(tc, qT, k_words, k_scales, kb, bd, offs, ou
         offsets = keep.tile([P, N // 16], U16, name="offsets")
         nc.sync.dma_start(offsets[:], offs)
 
-        bd_cols = keep.tile([P, 4 * SPREAD_BANKS], F32, name="bd_cols")
-        nc.sync.dma_start(out=bd_cols[:], in_=bd[0, LOADED:T].rearrange("(p j) -> p j", p=P))
-
         scale_win = keep.tile([P, T], U8, name="scale_win", tag="scales_then_q_codes", align_bytes=64)
         nc.vector.memset(scale_win[:].bitcast(I32), 0)
-        warm_in = keep.tile([P, 1], F32, name="warm_in")
-        nc.gpsimd.memset(warm_in[:], 0.0)
-        kb_win = keep.tile([P, T], F32, name="kb_win", tag="bias_then_scales", align_bytes=64)
+        kb_win = keep.tile([P, T], F32, name="kb_win", tag="row_window")
         nc.sync.dma_start(out=kb_win[P - 1 : P, :], in_=kb[0:1, :])
-        nc.vector.memset(kb_win[0 : P - 1, :].bitcast(I32), 0)
+        q_raw = keep.tile([P, PACK, NQ], F32, name="q_raw")
+        nc.sync.dma_start(out=q_raw[:], in_=qT[0].rearrange("(p j) w -> p j w", j=PACK))
+
+        warm = keep.tile([P, 1], F32, name="warm")
+        nc.gpsimd.memset(warm[:], 0.0)
+        nc.scalar.activation(warm[:], warm[:], ACT.Sigmoid)
+        zeros = keep.tile([P, P], F32, name="zeros", tag="zeros_then_words")
+        nc.gpsimd.memset(zeros[:], 0.0)
+        ident = keep.tile([P, P], F32, name="ident")
+        nc.gpsimd.affine_select(
+            out=ident[:], in_=zeros[:], compare_op=ALU.not_equal, fill=1.0, base=0, pattern=[[-1, P]], channel_multiplier=1
+        )
+        kb_zero = kb_win[0 : P - 1, :].bitcast(I32)
+        nc.vector.memset(kb_zero[:, 0 : T // 2], 0)
+        nc.vector.memset(kb_zero[:, T // 2 : T], 0)
 
         scale_rows = k_scales[0].bitcast(I32)
         for r in range(4):
             nc.sync.dma_start(out=scale_win[:].bitcast(I32)[r:P:32, :], in_=scale_rows[r:16:4, :])
+        word_win = keep.tile([P, T], I32, name="word_win", tag="zeros_then_words")
+        nc.sync.dma_start(out=word_win[:], in_=k_words[0].rearrange("p n t -> p (n t)").bitcast(I32))
 
-        q_raw = keep.tile([P, PACK, NQ], F32, name="q_raw")
-        nc.scalar.dma_start(out=q_raw[:], in_=qT[0].rearrange("(p j) w -> p j w", j=PACK))
-        word_win = keep.tile([P, T], I32, name="word_win", tag="words_then_bids")
-        nc.scalar.dma_start(out=word_win[:], in_=k_words[0].rearrange("p n t -> p (n t)").bitcast(I32))
-
-        ident = keep.tile([P, P], F32, name="ident")
-        make_identity(nc, ident[:])
-        warm = keep.tile([P, 1], F32, name="warm")
-        nc.scalar.activation(warm[:], warm_in[:], ACT.Sigmoid)
-
-        bd_win = keep.tile([P, T], F32, name="bd_win")
-        bd_by_run = bd_win[:, LOADED:T].rearrange("r (p b i) -> r p b i", p=P, i=4)
-        for b in range(SPREAD_BANKS):
-            spread = turn_psum.tile([P, 4, P], F32, name="spread", tag="turn")
-            for i in range(4):
-                c = 4 * b + i
-                nc.tensor.transpose(spread[:, i, :], bd_cols[:, c : c + 1].to_broadcast([P, P]), ident[:])
-            nc.scalar.copy(out=bd_by_run[:, :, b, :], in_=spread[:].rearrange("r i p -> r p i"))
 
         kb_g = keep.tile([P, N], F32, name="kb_g")
         nc.vector.tensor_copy(kb_g[:], kb_win[:].indirect(offsets[:]))
-        scale_g = keep.tile([P, N], U8, name="scale_g", tag="bias_then_scales", align_bytes=64)
+        scale_g = keep.tile([P, N], U8, name="scale_g", align_bytes=64)
         nc.vector.tensor_copy(scale_g[:], scale_win[:].indirect(offsets[:]))
 
-        q_grp = keep.tile([P, NQ, PACK], BF16, name="q_grp", tag="q_then_words", align_bytes=64)
+        q_grp = keep.tile([P, NQ, PACK], BF16, name="q_grp", align_bytes=64)
         nc.scalar.copy(
             out=q_grp[:].rearrange("p (c i) t -> p c t i", i=4),
             in_=q_raw[:].rearrange("p t (c i) -> p c t i", i=4),
         )
+        bd_win = keep.tile([P, T], F32, name="bd_win", tag="row_window")
+        nc.scalar.dma_start(out=bd_win[:], in_=bd)
         q_codes = keep.tile([P, NQ], U32, name="q_codes", tag="scales_then_q_codes", align_bytes=64)
         q_scales = keep.tile([P, NQ], U8, name="q_scales", align_bytes=64)
         nc.vector.quantize_mx(out=q_codes[:].bitcast(FP8X4), scales=q_scales[:], in_=q_grp[:].rearrange("p w j -> p (w j)"))
@@ -92,18 +84,16 @@ def tile_attend_link_bid_topk_kernel(tc, qT, k_words, k_scales, kb, bd, offs, ou
         kb_col = keep.tile([P, SLOT_TILES], F32, name="kb_col")
         nc.scalar.copy(out=kb_col[:], in_=kb_turned[:, :, P - 1])
 
-        word_g = keep.tile([P, N], U32, name="word_g", tag="q_then_words", align_bytes=64)
+        word_g = [keep.tile([P, HALF], U32, name="word_g%d" % h, align_bytes=64) for h in range(2)]
         for h in range(2):
-            nc.vector.tensor_copy(word_g[:, h * HALF : (h + 1) * HALF], word_win[:].bitcast(U32).indirect(offsets[:, h * 16 : (h + 1) * 16]))
-        bd_g = keep.tile([P, N], F32, name="bd_g", tag="words_then_bids")
-        nc.vector.tensor_copy(bd_g[:], bd_win[:].indirect(offsets[:]))
+            nc.vector.tensor_copy(word_g[h][:], word_win[:].bitcast(U32).indirect(offsets[:, h * 16 : (h + 1) * 16]))
 
         probs = []
         for j in range(SLOT_TILES):
             score = score_psum.tile([P, NQ], F32, name="score", tag="score")
             nc.tensor.matmul_mx(
                 out=score[:],
-                lhsT=word_g[:, j * P : (j + 1) * P].bitcast(FP8X4),
+                lhsT=word_g[j // 2][:, (j % 2) * P : (j % 2 + 1) * P].bitcast(FP8X4),
                 lhsT_scale=scale_g[:, j * P : (j + 1) * P],
                 rhs=q_codes[:].bitcast(FP8X4),
                 rhs_scale=q_scales[:],
@@ -115,6 +105,8 @@ def tile_attend_link_bid_topk_kernel(tc, qT, k_words, k_scales, kb, bd, offs, ou
             probs.append(prob)
 
         out_v = out[0].rearrange("(u p) n -> p u n", p=P)
+        bd_g = keep.tile([P, N], F32, name="bd_g", tag="zeros_then_words")
+        nc.vector.tensor_copy(bd_g[:], bd_win[:].indirect(offsets[:]))
         for j in range(SLOT_TILES):
             turned = turn_psum.tile([P, Q_TILES, P], F32, name="turned", tag="turn")
             for u in range(Q_TILES):

@@ -18,9 +18,14 @@ T = 2048
 N = 512
 NQ = 256
 D = 512
+QUADRANT = 32
+SCALE_ROWS = 4
+LIST_ROWS = 16
 SLOT_TILES = N // P
 Q_TILES = NQ // P
 HALF = N // 2
+WINDOW_BYTES = 4 * T
+ZEROS_BYTES = 4 * P
 
 FLOPS = 2 * D * NQ * N
 
@@ -29,24 +34,25 @@ def tile_attend_link_bid_topk_kernel(tc, qT, k_words, k_scales, kb, bd, offs, ou
     nc = tc.nc
     with ExitStack() as ctx:
         keep = ctx.enter_context(tc.tile_pool(name="keep", bufs=1))
+        shared = ctx.enter_context(tc.tile_pool(name="shared", bufs=1))
         score_psum = ctx.enter_context(tc.psum_pool(name="score_psum", bufs=SLOT_TILES))
         turn_psum = ctx.enter_context(tc.psum_pool(name="turn_psum", bufs=SLOT_TILES))
 
-        offsets = keep.tile([P, N // 16], U16, name="offsets")
+        offsets = keep.tile([P, N // LIST_ROWS], U16, name="offsets")
         nc.sync.dma_start(offsets[:], offs)
 
         scale_win = keep.tile([P, T], U8, name="scale_win", tag="scales_then_q_codes", align_bytes=64)
         nc.vector.memset(scale_win[:].bitcast(I32), 0)
-        kb_win = keep.tile([P, T], F32, name="kb_win", tag="row_window")
-        nc.sync.dma_start(out=kb_win[P - 1 : P, :], in_=kb[0:1, :])
+        kb_win = keep.tile([P, T], F32, name="kb_win")
+        nc.scalar.dma_start(out=kb_win[P - 1 : P, :], in_=kb[0:1, :])
         q_raw = keep.tile([P, PACK, NQ], F32, name="q_raw")
         nc.sync.dma_start(out=q_raw[:], in_=qT[0].rearrange("(p j) w -> p j w", j=PACK))
 
+        zeros = shared.tile([P, P], F32, name="zeros", offset=WINDOW_BYTES - ZEROS_BYTES // 2)
+        nc.gpsimd.memset(zeros[:], 0.0)
         warm = keep.tile([P, 1], F32, name="warm")
         nc.gpsimd.memset(warm[:], 0.0)
         nc.scalar.activation(warm[:], warm[:], ACT.Sigmoid)
-        zeros = keep.tile([P, P], F32, name="zeros", tag="zeros_then_words")
-        nc.gpsimd.memset(zeros[:], 0.0)
         ident = keep.tile([P, P], F32, name="ident")
         nc.gpsimd.affine_select(
             out=ident[:], in_=zeros[:], compare_op=ALU.not_equal, fill=1.0, base=0, pattern=[[-1, P]], channel_multiplier=1
@@ -56,11 +62,14 @@ def tile_attend_link_bid_topk_kernel(tc, qT, k_words, k_scales, kb, bd, offs, ou
         nc.vector.memset(kb_zero[:, T // 2 : T], 0)
 
         scale_rows = k_scales[0].bitcast(I32)
-        for r in range(4):
-            nc.sync.dma_start(out=scale_win[:].bitcast(I32)[r:P:32, :], in_=scale_rows[r:16:4, :])
-        word_win = keep.tile([P, T], I32, name="word_win", tag="zeros_then_words")
+        for r in range(SCALE_ROWS):
+            nc.sync.dma_start(
+                out=scale_win[:].bitcast(I32)[r:P:QUADRANT, :], in_=scale_rows[r : D // 32 : SCALE_ROWS, :]
+            )
+        word_win = shared.tile([P, T], I32, name="word_win", offset=0)
         nc.sync.dma_start(out=word_win[:], in_=k_words[0].rearrange("p n t -> p (n t)").bitcast(I32))
-
+        bd_win = shared.tile([P, T], F32, name="bd_win", offset=WINDOW_BYTES)
+        nc.sync.dma_start(out=bd_win[:], in_=bd)
 
         kb_g = keep.tile([P, N], F32, name="kb_g")
         nc.vector.tensor_copy(kb_g[:], kb_win[:].indirect(offsets[:]))
@@ -72,11 +81,11 @@ def tile_attend_link_bid_topk_kernel(tc, qT, k_words, k_scales, kb, bd, offs, ou
             out=q_grp[:].rearrange("p (c i) t -> p c t i", i=4),
             in_=q_raw[:].rearrange("p t (c i) -> p c t i", i=4),
         )
-        bd_win = keep.tile([P, T], F32, name="bd_win", tag="row_window")
-        nc.scalar.dma_start(out=bd_win[:], in_=bd)
         q_codes = keep.tile([P, NQ], U32, name="q_codes", tag="scales_then_q_codes", align_bytes=64)
         q_scales = keep.tile([P, NQ], U8, name="q_scales", align_bytes=64)
-        nc.vector.quantize_mx(out=q_codes[:].bitcast(FP8X4), scales=q_scales[:], in_=q_grp[:].rearrange("p w j -> p (w j)"))
+        nc.vector.quantize_mx(
+            out=q_codes[:].bitcast(FP8X4), scales=q_scales[:], in_=q_grp[:].rearrange("p w j -> p (w j)")
+        )
 
         kb_turned = turn_psum.tile([P, SLOT_TILES, P], F32, name="kb_turned", tag="turn")
         for j in range(SLOT_TILES):
@@ -84,16 +93,19 @@ def tile_attend_link_bid_topk_kernel(tc, qT, k_words, k_scales, kb, bd, offs, ou
         kb_col = keep.tile([P, SLOT_TILES], F32, name="kb_col")
         nc.scalar.copy(out=kb_col[:], in_=kb_turned[:, :, P - 1])
 
-        word_g = [keep.tile([P, HALF], U32, name="word_g%d" % h, align_bytes=64) for h in range(2)]
-        for h in range(2):
-            nc.vector.tensor_copy(word_g[h][:], word_win[:].bitcast(U32).indirect(offsets[:, h * 16 : (h + 1) * 16]))
+        word_g = [keep.tile([P, HALF], U32, name="word_g%d" % h, align_bytes=64) for h in range(N // HALF)]
+        list_cols = HALF // LIST_ROWS
+        for h in range(N // HALF):
+            half_list = offsets[:, h * list_cols : (h + 1) * list_cols]
+            nc.vector.tensor_copy(word_g[h][:], word_win[:].bitcast(U32).indirect(half_list))
 
         probs = []
         for j in range(SLOT_TILES):
+            h, first = divmod(j * P, HALF)
             score = score_psum.tile([P, NQ], F32, name="score", tag="score")
             nc.tensor.matmul_mx(
                 out=score[:],
-                lhsT=word_g[j // 2][:, (j % 2) * P : (j % 2 + 1) * P].bitcast(FP8X4),
+                lhsT=word_g[h][:, first : first + P].bitcast(FP8X4),
                 lhsT_scale=scale_g[:, j * P : (j + 1) * P],
                 rhs=q_codes[:].bitcast(FP8X4),
                 rhs_scale=q_scales[:],
@@ -105,14 +117,13 @@ def tile_attend_link_bid_topk_kernel(tc, qT, k_words, k_scales, kb, bd, offs, ou
             probs.append(prob)
 
         out_v = out[0].rearrange("(u p) n -> p u n", p=P)
-        bd_g = keep.tile([P, N], F32, name="bd_g", tag="zeros_then_words")
+        bd_g = shared.tile([P, N], F32, name="bd_g", offset=0)
         nc.vector.tensor_copy(bd_g[:], bd_win[:].indirect(offsets[:]))
         for j in range(SLOT_TILES):
             turned = turn_psum.tile([P, Q_TILES, P], F32, name="turned", tag="turn")
             for u in range(Q_TILES):
                 nc.tensor.transpose(turned[:, u, :], probs[j][:, u * P : (u + 1) * P], ident[:])
             res = keep.tile([P, Q_TILES, P], F32, name="res%d" % j)
-            nc.vector.tensor_tensor(
-                res[:], turned[:], bd_g[:, j * P : (j + 1) * P].unsqueeze(1).to_broadcast([P, Q_TILES, P]), ALU.mult
-            )
+            bids = bd_g[:, j * P : (j + 1) * P].unsqueeze(1).to_broadcast([P, Q_TILES, P])
+            nc.vector.tensor_tensor(res[:], turned[:], bids, ALU.mult)
             nc.sync.dma_start(out=out_v[:, :, j * P : (j + 1) * P], in_=res[:])

@@ -26,6 +26,8 @@ Q_TILES = NQ // P
 HALF = N // 2
 WINDOW_BYTES = 4 * T
 ZEROS_BYTES = 4 * P
+BID_COLS = T // P
+BANK_TILES = 4
 
 FLOPS = 2 * D * NQ * N
 
@@ -45,10 +47,12 @@ def tile_attend_link_bid_topk_kernel(tc, qT, k_words, k_scales, kb, bd, offs, ou
         nc.vector.memset(scale_win[:].bitcast(I32), 0)
         kb_win = keep.tile([P, T], F32, name="kb_win")
         nc.scalar.dma_start(out=kb_win[P - 1 : P, :], in_=kb[0:1, :])
+        bd_cols = keep.tile([P, BID_COLS], F32, name="bd_cols")
+        nc.sync.dma_start(out=bd_cols[:], in_=bd[0].rearrange("(p c) -> p c", c=BID_COLS))
         q_raw = keep.tile([P, PACK, NQ], F32, name="q_raw")
         nc.sync.dma_start(out=q_raw[:], in_=qT[0].rearrange("(p j) w -> p j w", j=PACK))
 
-        zeros = shared.tile([P, P], F32, name="zeros", offset=WINDOW_BYTES - ZEROS_BYTES // 2)
+        zeros = shared.tile([P, P], F32, name="zeros", offset=WINDOW_BYTES - ZEROS_BYTES)
         nc.gpsimd.memset(zeros[:], 0.0)
         warm = keep.tile([P, 1], F32, name="warm")
         nc.gpsimd.memset(warm[:], 0.0)
@@ -68,8 +72,15 @@ def tile_attend_link_bid_topk_kernel(tc, qT, k_words, k_scales, kb, bd, offs, ou
             )
         word_win = shared.tile([P, T], I32, name="word_win", offset=0)
         nc.sync.dma_start(out=word_win[:], in_=k_words[0].rearrange("p n t -> p (n t)").bitcast(I32))
-        bd_win = shared.tile([P, T], F32, name="bd_win", offset=WINDOW_BYTES)
-        nc.sync.dma_start(out=bd_win[:], in_=bd)
+
+        bd_win = keep.tile([P, T], F32, name="bd_win")
+        bd_win_v = bd_win[:].rearrange("p (n b c) -> p b n c", b=BID_COLS // BANK_TILES, c=BANK_TILES)
+        for b in range(BID_COLS // BANK_TILES):
+            spread = score_psum.tile([P, BANK_TILES, P], F32, name="spread", tag="score")
+            for c in range(BANK_TILES):
+                col = b * BANK_TILES + c
+                nc.tensor.transpose(spread[:, c, :], bd_cols[:, col : col + 1].to_broadcast([P, P]), ident[:])
+            nc.scalar.copy(out=bd_win_v[:, b], in_=spread[:].rearrange("p c n -> p n c"))
 
         kb_g = keep.tile([P, N], F32, name="kb_g")
         nc.vector.tensor_copy(kb_g[:], kb_win[:].indirect(offsets[:]))

@@ -23,11 +23,8 @@ SCALE_ROWS = 4
 LIST_ROWS = 16
 SLOT_TILES = N // P
 Q_TILES = NQ // P
-HALF = N // 2
-WINDOW_BYTES = 4 * T
-ZEROS_BYTES = 4 * P
-BID_COLS = T // P
-BANK_TILES = 4
+HALVES = 2
+HALF = N // HALVES
 
 FLOPS = 2 * D * NQ * N
 
@@ -36,24 +33,23 @@ def tile_attend_link_bid_topk_kernel(tc, qT, k_words, k_scales, kb, bd, offs, ou
     nc = tc.nc
     with ExitStack() as ctx:
         keep = ctx.enter_context(tc.tile_pool(name="keep", bufs=1))
-        shared = ctx.enter_context(tc.tile_pool(name="shared", bufs=1))
-        score_psum = ctx.enter_context(tc.psum_pool(name="score_psum", bufs=SLOT_TILES))
-        turn_psum = ctx.enter_context(tc.psum_pool(name="turn_psum", bufs=SLOT_TILES))
+        psum = ctx.enter_context(tc.psum_pool(name="psum", bufs=1))
 
         offsets = keep.tile([P, N // LIST_ROWS], U16, name="offsets")
         nc.sync.dma_start(offsets[:], offs)
-
-        scale_win = keep.tile([P, T], U8, name="scale_win", tag="scales_then_q_codes", align_bytes=64)
-        nc.vector.memset(scale_win[:].bitcast(I32), 0)
         kb_win = keep.tile([P, T], F32, name="kb_win")
         nc.scalar.dma_start(out=kb_win[P - 1 : P, :], in_=kb[0:1, :])
-        bd_cols = keep.tile([P, BID_COLS], F32, name="bd_cols")
-        nc.sync.dma_start(out=bd_cols[:], in_=bd[0].rearrange("(p c) -> p c", c=BID_COLS))
+        bd_win = keep.tile([P, T], F32, name="bd_win")
+        nc.sync.dma_start(out=bd_win[P - 1 : P, :], in_=bd[0:1, :])
         q_raw = keep.tile([P, PACK, NQ], F32, name="q_raw")
         nc.sync.dma_start(out=q_raw[:], in_=qT[0].rearrange("(p j) w -> p j w", j=PACK))
 
-        zeros = shared.tile([P, P], F32, name="zeros", offset=WINDOW_BYTES - ZEROS_BYTES)
-        nc.gpsimd.memset(zeros[:], 0.0)
+        scale_win = keep.tile([P, T], U8, name="scale_win", tag="scales_then_q_codes", align_bytes=64)
+        nc.vector.memset(scale_win[:].bitcast(I32), 0)
+        nc.vector.memset(kb_win[0 : P - 1, :].bitcast(I32), 0)
+        zeros = keep.tile([P, P], F32, name="zeros")
+        nc.vector.memset(zeros[:], 0.0)
+        nc.vector.memset(bd_win[0 : P - 1, :].bitcast(I32), 0)
         warm = keep.tile([P, 1], F32, name="warm")
         nc.gpsimd.memset(warm[:], 0.0)
         nc.scalar.activation(warm[:], warm[:], ACT.Sigmoid)
@@ -61,31 +57,37 @@ def tile_attend_link_bid_topk_kernel(tc, qT, k_words, k_scales, kb, bd, offs, ou
         nc.gpsimd.affine_select(
             out=ident[:], in_=zeros[:], compare_op=ALU.not_equal, fill=1.0, base=0, pattern=[[-1, P]], channel_multiplier=1
         )
-        kb_zero = kb_win[0 : P - 1, :].bitcast(I32)
-        nc.vector.memset(kb_zero[:, 0 : T // 2], 0)
-        nc.vector.memset(kb_zero[:, T // 2 : T], 0)
 
         scale_rows = k_scales[0].bitcast(I32)
         for r in range(SCALE_ROWS):
             nc.sync.dma_start(
                 out=scale_win[:].bitcast(I32)[r:P:QUADRANT, :], in_=scale_rows[r : D // 32 : SCALE_ROWS, :]
             )
-        word_win = shared.tile([P, T], I32, name="word_win", offset=0)
+        word_win = keep.tile([P, T], I32, name="word_win")
         nc.sync.dma_start(out=word_win[:], in_=k_words[0].rearrange("p n t -> p (n t)").bitcast(I32))
 
-        bd_win = keep.tile([P, T], F32, name="bd_win")
-        bd_win_v = bd_win[:].rearrange("p (n b c) -> p b n c", b=BID_COLS // BANK_TILES, c=BANK_TILES)
-        for b in range(BID_COLS // BANK_TILES):
-            spread = score_psum.tile([P, BANK_TILES, P], F32, name="spread", tag="score")
-            for c in range(BANK_TILES):
-                col = b * BANK_TILES + c
-                nc.tensor.transpose(spread[:, c, :], bd_cols[:, col : col + 1].to_broadcast([P, P]), ident[:])
-            nc.scalar.copy(out=bd_win_v[:, b], in_=spread[:].rearrange("p c n -> p n c"))
-
         kb_g = keep.tile([P, N], F32, name="kb_g")
-        nc.vector.tensor_copy(kb_g[:], kb_win[:].indirect(offsets[:]))
+        nc.scalar.activation(kb_g[:], kb_win[:].indirect(offsets[:]), ACT.Copy)
+        bd_g = keep.tile([P, N], F32, name="bd_g")
+        nc.vector.tensor_copy(bd_g[:], bd_win[:].indirect(offsets[:]))
         scale_g = keep.tile([P, N], U8, name="scale_g", align_bytes=64)
         nc.vector.tensor_copy(scale_g[:], scale_win[:].indirect(offsets[:]))
+
+        rows = {"kb": kb_g, "bd": bd_g}
+        cols, wide = {}, {}
+        for name, row in rows.items():
+            turned = psum.tile([P, SLOT_TILES, P], F32, name=name + "_turned")
+            for j in range(SLOT_TILES):
+                nc.tensor.transpose(turned[:, j, :], row[:, j * P : (j + 1) * P], ident[:])
+            cols[name] = keep.tile([P, SLOT_TILES], F32, name=name + "_col")
+            nc.scalar.copy(out=cols[name][:], in_=turned[:, :, P - 1])
+        for name in rows:
+            wide[name] = psum.tile([P, SLOT_TILES, P], F32, name=name + "_wide")
+            for j in range(SLOT_TILES):
+                nc.tensor.transpose(wide[name][:, j, :], cols[name][:, j : j + 1].to_broadcast([P, P]), ident[:])
+        kb_all = keep.tile([P, SLOT_TILES, P], F32, name="kb_all")
+        nc.scalar.copy(out=kb_all[:], in_=wide["kb"][:])
+        bd_wide = wide["bd"]
 
         q_grp = keep.tile([P, NQ, PACK], BF16, name="q_grp", align_bytes=64)
         nc.scalar.copy(
@@ -98,43 +100,37 @@ def tile_attend_link_bid_topk_kernel(tc, qT, k_words, k_scales, kb, bd, offs, ou
             out=q_codes[:].bitcast(FP8X4), scales=q_scales[:], in_=q_grp[:].rearrange("p w j -> p (w j)")
         )
 
-        kb_turned = turn_psum.tile([P, SLOT_TILES, P], F32, name="kb_turned", tag="turn")
-        for j in range(SLOT_TILES):
-            nc.tensor.transpose(kb_turned[:, j, :], kb_g[:, j * P : (j + 1) * P], ident[:])
-        kb_col = keep.tile([P, SLOT_TILES], F32, name="kb_col")
-        nc.scalar.copy(out=kb_col[:], in_=kb_turned[:, :, P - 1])
-
-        word_g = [keep.tile([P, HALF], U32, name="word_g%d" % h, align_bytes=64) for h in range(N // HALF)]
         list_cols = HALF // LIST_ROWS
-        for h in range(N // HALF):
-            half_list = offsets[:, h * list_cols : (h + 1) * list_cols]
-            nc.vector.tensor_copy(word_g[h][:], word_win[:].bitcast(U32).indirect(half_list))
+        word_g = [keep.tile([P, HALF], U32, name="word_g%d" % h, align_bytes=64) for h in range(HALVES)]
+        for h in range(HALVES):
+            nc.vector.tensor_copy(
+                word_g[h][:], word_win[:].bitcast(U32).indirect(offsets[:, h * list_cols : (h + 1) * list_cols])
+            )
 
+        pieces = [(h, u) for h in range(HALVES) for u in range(Q_TILES)]
+        kb_row = kb_all[:].rearrange("p j s -> p (j s)")
+        bd_row = bd_wide[:].rearrange("p j s -> p (j s)")
         probs = []
-        for j in range(SLOT_TILES):
-            h, first = divmod(j * P, HALF)
-            score = score_psum.tile([P, NQ], F32, name="score", tag="score")
+        for h, u in pieces:
+            slots = slice(h * HALF, (h + 1) * HALF)
+            score = psum.tile([P, HALF], F32, name="score%d%d" % (h, u))
             nc.tensor.matmul_mx(
                 out=score[:],
-                lhsT=word_g[h][:, first : first + P].bitcast(FP8X4),
-                lhsT_scale=scale_g[:, j * P : (j + 1) * P],
-                rhs=q_codes[:].bitcast(FP8X4),
-                rhs_scale=q_scales[:],
+                lhsT=q_codes[:, u * P : (u + 1) * P].bitcast(FP8X4),
+                lhsT_scale=q_scales[:, u * P : (u + 1) * P],
+                rhs=word_g[h][:].bitcast(FP8X4),
+                rhs_scale=scale_g[:, slots],
                 start=True,
                 stop=True,
             )
-            prob = keep.tile([P, NQ], F32, name="prob%d" % j)
-            nc.scalar.activation(prob[:], score[:], ACT.Sigmoid, bias=kb_col[:, j : j + 1])
+            logit = keep.tile([P, HALF], F32, name="logit%d%d" % (h, u))
+            nc.vector.tensor_tensor(logit[:], score[:], kb_row[:, slots], ALU.add)
+            prob = keep.tile([P, HALF], F32, name="prob%d%d" % (h, u))
+            nc.scalar.activation(prob[:], logit[:], ACT.Sigmoid)
             probs.append(prob)
 
-        out_v = out[0].rearrange("(u p) n -> p u n", p=P)
-        bd_g = shared.tile([P, N], F32, name="bd_g", offset=0)
-        nc.vector.tensor_copy(bd_g[:], bd_win[:].indirect(offsets[:]))
-        for j in range(SLOT_TILES):
-            turned = turn_psum.tile([P, Q_TILES, P], F32, name="turned", tag="turn")
-            for u in range(Q_TILES):
-                nc.tensor.transpose(turned[:, u, :], probs[j][:, u * P : (u + 1) * P], ident[:])
-            res = keep.tile([P, Q_TILES, P], F32, name="res%d" % j)
-            bids = bd_g[:, j * P : (j + 1) * P].unsqueeze(1).to_broadcast([P, Q_TILES, P])
-            nc.vector.tensor_tensor(res[:], turned[:], bids, ALU.mult)
-            nc.sync.dma_start(out=out_v[:, :, j * P : (j + 1) * P], in_=res[:])
+        for (h, u), prob in zip(pieces, probs):
+            slots = slice(h * HALF, (h + 1) * HALF)
+            res = keep.tile([P, HALF], F32, name="res%d%d" % (h, u))
+            nc.vector.tensor_tensor(res[:], prob[:], bd_row[:, slots], ALU.mult)
+            nc.sync.dma_start(out=out[0, u * P : (u + 1) * P, slots], in_=res[:])

@@ -25,6 +25,7 @@ SLOT_TILES = N // P
 Q_TILES = NQ // P
 HALVES = 2
 HALF = N // HALVES
+BIDS_ON_VECTOR = 256
 
 FLOPS = 2 * D * NQ * N
 
@@ -44,7 +45,7 @@ def tile_attend_link_bid_topk_kernel(tc, qT, k_words, k_scales, kb, bd, offs, ou
         q_raw = keep.tile([P, PACK, NQ], F32, name="q_raw")
         nc.sync.dma_start(out=q_raw[:], in_=qT[0].rearrange("(p j) w -> p j w", j=PACK))
 
-        scale_win = keep.tile([P, T], U8, name="scale_win", tag="scales_then_q_codes", align_bytes=64)
+        scale_win = keep.tile([P, T], U8, name="scale_win", align_bytes=64)
         nc.vector.memset(scale_win[:].bitcast(I32), 0)
         nc.vector.memset(kb_win[0 : P - 1, :].bitcast(I32), 0)
         zeros = keep.tile([P, P], F32, name="zeros")
@@ -68,17 +69,36 @@ def tile_attend_link_bid_topk_kernel(tc, qT, k_words, k_scales, kb, bd, offs, ou
 
         kb_g = keep.tile([P, N], F32, name="kb_g")
         nc.scalar.activation(kb_g[:], kb_win[:].indirect(offsets[:]), ACT.Copy)
-        bd_g = keep.tile([P, N], F32, name="bd_g")
-        nc.vector.tensor_copy(bd_g[:], bd_win[:].indirect(offsets[:]))
+        split = BIDS_ON_VECTOR // LIST_ROWS
+        bd_first = keep.tile([P, BIDS_ON_VECTOR], F32, name="bd_first")
+        nc.vector.tensor_copy(bd_first[:], bd_win[:].indirect(offsets[:, 0:split]))
+        bd_rest = keep.tile([P, N - BIDS_ON_VECTOR], F32, name="bd_rest")
+        nc.scalar.activation(bd_rest[:], bd_win[:].indirect(offsets[:, split : N // LIST_ROWS]), ACT.Copy)
+        q_grp = [keep.tile([P, P, PACK], BF16, name="q_grp%d" % u, align_bytes=64) for u in range(Q_TILES)]
+        q_codes = [keep.tile([P, P], U32, name="q_codes%d" % u, align_bytes=64) for u in range(Q_TILES)]
+        q_scales = [keep.tile([P, P], U8, name="q_scales%d" % u, align_bytes=64) for u in range(Q_TILES)]
+        for u in range(Q_TILES):
+            nc.vector.tensor_copy(
+                out=q_grp[u][:].rearrange("p (c i) t -> p c t i", i=4),
+                in_=q_raw[:, :, u * P : (u + 1) * P].rearrange("p t (c i) -> p c t i", i=4),
+            )
+        for u in range(Q_TILES):
+            nc.vector.quantize_mx(
+                out=q_codes[u][:].bitcast(FP8X4), scales=q_scales[u][:], in_=q_grp[u][:].rearrange("p w j -> p (w j)")
+            )
         scale_g = keep.tile([P, N], U8, name="scale_g", align_bytes=64)
         nc.vector.tensor_copy(scale_g[:], scale_win[:].indirect(offsets[:]))
 
-        rows = {"kb": kb_g, "bd": bd_g}
+        rows = {
+            "kb": [kb_g[:, j * P : (j + 1) * P] for j in range(SLOT_TILES)],
+            "bd": [bd_first[:, s : s + P] for s in range(0, BIDS_ON_VECTOR, P)]
+            + [bd_rest[:, s : s + P] for s in range(0, N - BIDS_ON_VECTOR, P)],
+        }
         cols, wide = {}, {}
         for name, row in rows.items():
             turned = psum.tile([P, SLOT_TILES, P], F32, name=name + "_turned")
             for j in range(SLOT_TILES):
-                nc.tensor.transpose(turned[:, j, :], row[:, j * P : (j + 1) * P], ident[:])
+                nc.tensor.transpose(turned[:, j, :], row[j], ident[:])
             cols[name] = keep.tile([P, SLOT_TILES], F32, name=name + "_col")
             nc.scalar.copy(out=cols[name][:], in_=turned[:, :, P - 1])
         for name in rows:
@@ -88,17 +108,6 @@ def tile_attend_link_bid_topk_kernel(tc, qT, k_words, k_scales, kb, bd, offs, ou
         kb_all = keep.tile([P, SLOT_TILES, P], F32, name="kb_all")
         nc.scalar.copy(out=kb_all[:], in_=wide["kb"][:])
         bd_wide = wide["bd"]
-
-        q_grp = keep.tile([P, NQ, PACK], BF16, name="q_grp", align_bytes=64)
-        nc.scalar.copy(
-            out=q_grp[:].rearrange("p (c i) t -> p c t i", i=4),
-            in_=q_raw[:].rearrange("p t (c i) -> p c t i", i=4),
-        )
-        q_codes = keep.tile([P, NQ], U32, name="q_codes", tag="scales_then_q_codes", align_bytes=64)
-        q_scales = keep.tile([P, NQ], U8, name="q_scales", align_bytes=64)
-        nc.vector.quantize_mx(
-            out=q_codes[:].bitcast(FP8X4), scales=q_scales[:], in_=q_grp[:].rearrange("p w j -> p (w j)")
-        )
 
         list_cols = HALF // LIST_ROWS
         word_g = [keep.tile([P, HALF], U32, name="word_g%d" % h, align_bytes=64) for h in range(HALVES)]
@@ -116,8 +125,8 @@ def tile_attend_link_bid_topk_kernel(tc, qT, k_words, k_scales, kb, bd, offs, ou
             score = psum.tile([P, HALF], F32, name="score%d%d" % (h, u))
             nc.tensor.matmul_mx(
                 out=score[:],
-                lhsT=q_codes[:, u * P : (u + 1) * P].bitcast(FP8X4),
-                lhsT_scale=q_scales[:, u * P : (u + 1) * P],
+                lhsT=q_codes[u][:].bitcast(FP8X4),
+                lhsT_scale=q_scales[u][:],
                 rhs=word_g[h][:].bitcast(FP8X4),
                 rhs_scale=scale_g[:, slots],
                 start=True,

@@ -25,7 +25,7 @@ SLOT_TILES = N // P
 Q_TILES = NQ // P
 HALVES = 2
 HALF = N // HALVES
-BIDS_ON_VECTOR = 256
+BIDS_ON_VECTOR = 128
 
 FLOPS = 2 * D * NQ * N
 

@@ -25,7 +25,6 @@ SLOT_TILES = N // P
 Q_TILES = NQ // P
 HALVES = 2
 HALF = N // HALVES
-BIDS_ON_VECTOR = 128
 
 FLOPS = 2 * D * NQ * N
 
@@ -67,13 +66,13 @@ def tile_attend_link_bid_topk_kernel(tc, qT, k_words, k_scales, kb, bd, offs, ou
         word_win = keep.tile([P, T], I32, name="word_win")
         nc.sync.dma_start(out=word_win[:], in_=k_words[0].rearrange("p n t -> p (n t)").bitcast(I32))
 
-        kb_g = keep.tile([P, N], F32, name="kb_g")
+        kb_g = keep.tile([P, N], F32, name="kb_g", tag="bias_then_last_bids")
         nc.scalar.activation(kb_g[:], kb_win[:].indirect(offsets[:]), ACT.Copy)
-        split = BIDS_ON_VECTOR // LIST_ROWS
-        bd_first = keep.tile([P, BIDS_ON_VECTOR], F32, name="bd_first")
-        nc.vector.tensor_copy(bd_first[:], bd_win[:].indirect(offsets[:, 0:split]))
-        bd_rest = keep.tile([P, N - BIDS_ON_VECTOR], F32, name="bd_rest")
-        nc.scalar.activation(bd_rest[:], bd_win[:].indirect(offsets[:, split : N // LIST_ROWS]), ACT.Copy)
+        tile_cols = P // LIST_ROWS
+        bd_first = keep.tile([P, P], F32, name="bd_first")
+        nc.vector.tensor_copy(bd_first[:], bd_win[:].indirect(offsets[:, 0:tile_cols]))
+        bd_middle = keep.tile([P, 2 * P], F32, name="bd_middle")
+        nc.scalar.activation(bd_middle[:], bd_win[:].indirect(offsets[:, tile_cols : 3 * tile_cols]), ACT.Copy)
         q_grp = [keep.tile([P, P, PACK], BF16, name="q_grp%d" % u, align_bytes=64) for u in range(Q_TILES)]
         q_codes = [keep.tile([P, P], U32, name="q_codes%d" % u, align_bytes=64) for u in range(Q_TILES)]
         q_scales = [keep.tile([P, P], U8, name="q_scales%d" % u, align_bytes=64) for u in range(Q_TILES)]
@@ -89,25 +88,30 @@ def tile_attend_link_bid_topk_kernel(tc, qT, k_words, k_scales, kb, bd, offs, ou
         scale_g = keep.tile([P, N], U8, name="scale_g", align_bytes=64)
         nc.vector.tensor_copy(scale_g[:], scale_win[:].indirect(offsets[:]))
 
-        rows = {
-            "kb": [kb_g[:, j * P : (j + 1) * P] for j in range(SLOT_TILES)],
-            "bd": [bd_first[:, s : s + P] for s in range(0, BIDS_ON_VECTOR, P)]
-            + [bd_rest[:, s : s + P] for s in range(0, N - BIDS_ON_VECTOR, P)],
-        }
-        cols, wide = {}, {}
-        for name, row in rows.items():
-            turned = psum.tile([P, SLOT_TILES, P], F32, name=name + "_turned")
-            for j in range(SLOT_TILES):
-                nc.tensor.transpose(turned[:, j, :], row[j], ident[:])
-            cols[name] = keep.tile([P, SLOT_TILES], F32, name=name + "_col")
-            nc.scalar.copy(out=cols[name][:], in_=turned[:, :, P - 1])
-        for name in rows:
-            wide[name] = psum.tile([P, SLOT_TILES, P], F32, name=name + "_wide")
-            for j in range(SLOT_TILES):
-                nc.tensor.transpose(wide[name][:, j, :], cols[name][:, j : j + 1].to_broadcast([P, P]), ident[:])
-        kb_all = keep.tile([P, SLOT_TILES, P], F32, name="kb_all")
-        nc.scalar.copy(out=kb_all[:], in_=wide["kb"][:])
-        bd_wide = wide["bd"]
+        def to_columns(tiles, name):
+            turned = psum.tile([P, len(tiles), P], F32, name=name + "_turned", tag=name + "_turned")
+            for j in range(len(tiles)):
+                nc.tensor.transpose(turned[:, j, :], tiles[j], ident[:])
+            col = keep.tile([P, len(tiles)], F32, name=name + "_col")
+            nc.scalar.copy(out=col[:], in_=turned[:, :, P - 1])
+            return col
+
+        def spread(bank, col):
+            for j in range(bank.shape[1] // P):
+                column = col[:, j : j + 1]
+                nc.tensor.transpose(bank[:, j * P : (j + 1) * P], column.to_broadcast([P, P]), ident[:])
+
+        kb_col = to_columns([kb_g[:, j * P : (j + 1) * P] for j in range(SLOT_TILES)], "kb")
+        kb_wide = psum.tile([P, N], F32, name="kb_wide")
+        spread(kb_wide, kb_col)
+        bd_last = keep.tile([P, P], F32, name="bd_last", tag="bias_then_last_bids")
+        nc.scalar.activation(bd_last[:], bd_win[:].indirect(offsets[:, 3 * tile_cols : 4 * tile_cols]), ACT.Copy)
+        bd_cols = [to_columns([bd_first[:], bd_middle[:, 0:P]], "bd0")]
+        bd_wide = [psum.tile([P, HALF], F32, name="bd_wide0", tag="kb_turned")]
+        spread(bd_wide[0], bd_cols[0])
+        kb_all = keep.tile([P, N], F32, name="kb_all")
+        nc.scalar.copy(out=kb_all[:], in_=kb_wide[:])
+        bd_cols.append(to_columns([bd_middle[:, P : 2 * P], bd_last[:]], "bd1"))
 
         list_cols = HALF // LIST_ROWS
         word_g = [keep.tile([P, HALF], U32, name="word_g%d" % h, align_bytes=64) for h in range(HALVES)]
@@ -117,12 +121,10 @@ def tile_attend_link_bid_topk_kernel(tc, qT, k_words, k_scales, kb, bd, offs, ou
             )
 
         pieces = [(h, u) for h in range(HALVES) for u in range(Q_TILES)]
-        kb_row = kb_all[:].rearrange("p j s -> p (j s)")
-        bd_row = bd_wide[:].rearrange("p j s -> p (j s)")
         probs = []
         for h, u in pieces:
             slots = slice(h * HALF, (h + 1) * HALF)
-            score = psum.tile([P, HALF], F32, name="score%d%d" % (h, u))
+            score = psum.tile([P, HALF], F32, name="score%d%d" % (h, u), tag="bank%d" % (h * Q_TILES + u))
             nc.tensor.matmul_mx(
                 out=score[:],
                 lhsT=q_codes[u][:].bitcast(FP8X4),
@@ -133,13 +135,15 @@ def tile_attend_link_bid_topk_kernel(tc, qT, k_words, k_scales, kb, bd, offs, ou
                 stop=True,
             )
             logit = keep.tile([P, HALF], F32, name="logit%d%d" % (h, u))
-            nc.vector.tensor_tensor(logit[:], score[:], kb_row[:, slots], ALU.add)
+            nc.vector.tensor_tensor(logit[:], score[:], kb_all[:, slots], ALU.add)
             prob = keep.tile([P, HALF], F32, name="prob%d%d" % (h, u))
             nc.scalar.activation(prob[:], logit[:], ACT.Sigmoid)
             probs.append(prob)
 
+        bd_wide.append(psum.tile([P, HALF], F32, name="bd_wide1", tag="bank0"))
+        spread(bd_wide[1], bd_cols[1])
         for (h, u), prob in zip(pieces, probs):
             slots = slice(h * HALF, (h + 1) * HALF)
             res = keep.tile([P, HALF], F32, name="res%d%d" % (h, u))
-            nc.vector.tensor_tensor(res[:], prob[:], bd_row[:, slots], ALU.mult)
+            nc.vector.tensor_tensor(res[:], prob[:], bd_wide[h][:], ALU.mult)
             nc.sync.dma_start(out=out[0, u * P : (u + 1) * P, slots], in_=res[:])

@@ -40,7 +40,7 @@ def tile_attend_link_bid_topk_kernel(tc, qT, k_words, k_scales, kb, bd, offs, ou
         kb_win = keep.tile([P, T], F32, name="kb_win")
         nc.scalar.dma_start(out=kb_win[P - 1 : P, :], in_=kb[0:1, :])
         bd_win = keep.tile([P, T], F32, name="bd_win")
-        nc.sync.dma_start(out=bd_win[P - 1 : P, :], in_=bd[0:1, :])
+        nc.scalar.dma_start(out=bd_win[P - 1 : P, :], in_=bd[0:1, :])
         q_raw = keep.tile([P, PACK, NQ], F32, name="q_raw")
         nc.sync.dma_start(out=q_raw[:], in_=qT[0].rearrange("(p j) w -> p j w", j=PACK))
 
@@ -66,13 +66,13 @@ def tile_attend_link_bid_topk_kernel(tc, qT, k_words, k_scales, kb, bd, offs, ou
         word_win = keep.tile([P, T], I32, name="word_win")
         nc.sync.dma_start(out=word_win[:], in_=k_words[0].rearrange("p n t -> p (n t)").bitcast(I32))
 
-        kb_g = keep.tile([P, N], F32, name="kb_g", tag="bias_then_last_bids")
-        nc.scalar.activation(kb_g[:], kb_win[:].indirect(offsets[:]), ACT.Copy)
         tile_cols = P // LIST_ROWS
-        bd_first = keep.tile([P, P], F32, name="bd_first")
-        nc.vector.tensor_copy(bd_first[:], bd_win[:].indirect(offsets[:, 0:tile_cols]))
-        bd_middle = keep.tile([P, 2 * P], F32, name="bd_middle")
-        nc.scalar.activation(bd_middle[:], bd_win[:].indirect(offsets[:, tile_cols : 3 * tile_cols]), ACT.Copy)
+        kb_first = keep.tile([P, 3 * P], F32, name="kb_first", tag="bias_then_last_bids")
+        nc.scalar.activation(kb_first[:], kb_win[:].indirect(offsets[:, 0 : 3 * tile_cols]), ACT.Copy)
+        kb_last = keep.tile([P, P], F32, name="kb_last")
+        nc.vector.tensor_copy(kb_last[:], kb_win[:].indirect(offsets[:, 3 * tile_cols : 4 * tile_cols]))
+        bd_first = keep.tile([P, 3 * P], F32, name="bd_first")
+        nc.scalar.activation(bd_first[:], bd_win[:].indirect(offsets[:, 0 : 3 * tile_cols]), ACT.Copy)
         q_grp = [keep.tile([P, P, PACK], BF16, name="q_grp%d" % u, align_bytes=64) for u in range(Q_TILES)]
         q_codes = [keep.tile([P, P], U32, name="q_codes%d" % u, align_bytes=64) for u in range(Q_TILES)]
         q_scales = [keep.tile([P, P], U8, name="q_scales%d" % u, align_bytes=64) for u in range(Q_TILES)]
@@ -101,17 +101,17 @@ def tile_attend_link_bid_topk_kernel(tc, qT, k_words, k_scales, kb, bd, offs, ou
                 column = col[:, j : j + 1]
                 nc.tensor.transpose(bank[:, j * P : (j + 1) * P], column.to_broadcast([P, P]), ident[:])
 
-        kb_col = to_columns([kb_g[:, j * P : (j + 1) * P] for j in range(SLOT_TILES)], "kb")
+        kb_col = to_columns([kb_first[:, j * P : (j + 1) * P] for j in range(3)] + [kb_last[:]], "kb")
         kb_wide = psum.tile([P, N], F32, name="kb_wide")
         spread(kb_wide, kb_col)
         bd_last = keep.tile([P, P], F32, name="bd_last", tag="bias_then_last_bids")
         nc.scalar.activation(bd_last[:], bd_win[:].indirect(offsets[:, 3 * tile_cols : 4 * tile_cols]), ACT.Copy)
-        bd_cols = [to_columns([bd_first[:], bd_middle[:, 0:P]], "bd0")]
+        bd_cols = [to_columns([bd_first[:, 0:P], bd_first[:, P : 2 * P]], "bd0")]
         bd_wide = [psum.tile([P, HALF], F32, name="bd_wide0", tag="kb_turned")]
         spread(bd_wide[0], bd_cols[0])
         kb_all = keep.tile([P, N], F32, name="kb_all")
         nc.scalar.copy(out=kb_all[:], in_=kb_wide[:])
-        bd_cols.append(to_columns([bd_middle[:, P : 2 * P], bd_last[:]], "bd1"))
+        bd_cols.append(to_columns([bd_first[:, 2 * P : 3 * P], bd_last[:]], "bd1"))
 
         list_cols = HALF // LIST_ROWS
         word_g = [keep.tile([P, HALF], U32, name="word_g%d" % h, align_bytes=64) for h in range(HALVES)]
@@ -121,10 +121,11 @@ def tile_attend_link_bid_topk_kernel(tc, qT, k_words, k_scales, kb, bd, offs, ou
             )
 
         pieces = [(h, u) for h in range(HALVES) for u in range(Q_TILES)]
+        score_tags = ["bd0_turned", "bd1_turned", "third_score", "last_score"]
         probs = []
         for h, u in pieces:
             slots = slice(h * HALF, (h + 1) * HALF)
-            score = psum.tile([P, HALF], F32, name="score%d%d" % (h, u), tag="bank%d" % (h * Q_TILES + u))
+            score = psum.tile([P, HALF], F32, name="score%d%d" % (h, u), tag=score_tags[h * Q_TILES + u])
             nc.tensor.matmul_mx(
                 out=score[:],
                 lhsT=q_codes[u][:].bitcast(FP8X4),
@@ -140,7 +141,7 @@ def tile_attend_link_bid_topk_kernel(tc, qT, k_words, k_scales, kb, bd, offs, ou
             nc.scalar.activation(prob[:], logit[:], ACT.Sigmoid)
             probs.append(prob)
 
-        bd_wide.append(psum.tile([P, HALF], F32, name="bd_wide1", tag="bank0"))
+        bd_wide.append(psum.tile([P, HALF], F32, name="bd_wide1", tag=score_tags[0]))
         spread(bd_wide[1], bd_cols[1])
         for (h, u), prob in zip(pieces, probs):
             slots = slice(h * HALF, (h + 1) * HALF)

@@ -40,7 +40,6 @@ def tile_attend_link_bid_topk_kernel(tc, qT, k_words, k_scales, kb, bd, offs, ou
         kb_win = keep.tile([P, T], F32, name="kb_win")
         nc.scalar.dma_start(out=kb_win[P - 1 : P, :], in_=kb[0:1, :])
         bd_win = keep.tile([P, T], F32, name="bd_win")
-        nc.scalar.dma_start(out=bd_win[P - 1 : P, :], in_=bd[0:1, :])
         q_raw = keep.tile([P, PACK, NQ], F32, name="q_raw")
         nc.sync.dma_start(out=q_raw[:], in_=qT[0].rearrange("(p j) w -> p j w", j=PACK))
 
@@ -63,6 +62,7 @@ def tile_attend_link_bid_topk_kernel(tc, qT, k_words, k_scales, kb, bd, offs, ou
             nc.sync.dma_start(
                 out=scale_win[:].bitcast(I32)[r:P:QUADRANT, :], in_=scale_rows[r : D // 32 : SCALE_ROWS, :]
             )
+        nc.sync.dma_start(out=bd_win[P - 1 : P, :], in_=bd[0:1, :])
         word_win = keep.tile([P, T], I32, name="word_win")
         nc.sync.dma_start(out=word_win[:], in_=k_words[0].rearrange("p n t -> p (n t)").bitcast(I32))
 
@@ -71,8 +71,8 @@ def tile_attend_link_bid_topk_kernel(tc, qT, k_words, k_scales, kb, bd, offs, ou
         nc.scalar.activation(kb_first[:], kb_win[:].indirect(offsets[:, 0 : 3 * tile_cols]), ACT.Copy)
         kb_last = keep.tile([P, P], F32, name="kb_last")
         nc.vector.tensor_copy(kb_last[:], kb_win[:].indirect(offsets[:, 3 * tile_cols : 4 * tile_cols]))
-        bd_first = keep.tile([P, 3 * P], F32, name="bd_first")
-        nc.scalar.activation(bd_first[:], bd_win[:].indirect(offsets[:, 0 : 3 * tile_cols]), ACT.Copy)
+        bd_first = keep.tile([P, HALF], F32, name="bd_first")
+        nc.scalar.activation(bd_first[:], bd_win[:].indirect(offsets[:, 0 : 2 * tile_cols]), ACT.Copy)
         q_grp = [keep.tile([P, P, PACK], BF16, name="q_grp%d" % u, align_bytes=64) for u in range(Q_TILES)]
         q_codes = [keep.tile([P, P], U32, name="q_codes%d" % u, align_bytes=64) for u in range(Q_TILES)]
         q_scales = [keep.tile([P, P], U8, name="q_scales%d" % u, align_bytes=64) for u in range(Q_TILES)]
@@ -104,14 +104,14 @@ def tile_attend_link_bid_topk_kernel(tc, qT, k_words, k_scales, kb, bd, offs, ou
         kb_col = to_columns([kb_first[:, j * P : (j + 1) * P] for j in range(3)] + [kb_last[:]], "kb")
         kb_wide = psum.tile([P, N], F32, name="kb_wide")
         spread(kb_wide, kb_col)
-        bd_last = keep.tile([P, P], F32, name="bd_last", tag="bias_then_last_bids")
-        nc.scalar.activation(bd_last[:], bd_win[:].indirect(offsets[:, 3 * tile_cols : 4 * tile_cols]), ACT.Copy)
+        bd_last = keep.tile([P, HALF], F32, name="bd_last", tag="bias_then_last_bids")
+        nc.scalar.activation(bd_last[:], bd_win[:].indirect(offsets[:, 2 * tile_cols : 4 * tile_cols]), ACT.Copy)
         bd_cols = [to_columns([bd_first[:, 0:P], bd_first[:, P : 2 * P]], "bd0")]
         bd_wide = [psum.tile([P, HALF], F32, name="bd_wide0", tag="kb_turned")]
         spread(bd_wide[0], bd_cols[0])
         kb_all = keep.tile([P, N], F32, name="kb_all")
         nc.scalar.copy(out=kb_all[:], in_=kb_wide[:])
-        bd_cols.append(to_columns([bd_first[:, 2 * P : 3 * P], bd_last[:]], "bd1"))
+        bd_cols.append(to_columns([bd_last[:, 0:P], bd_last[:, P : 2 * P]], "bd1"))
 
         list_cols = HALF // LIST_ROWS
         word_g = [keep.tile([P, HALF], U32, name="word_g%d" % h, align_bytes=64) for h in range(HALVES)]
@@ -121,7 +121,7 @@ def tile_attend_link_bid_topk_kernel(tc, qT, k_words, k_scales, kb, bd, offs, ou
             )
 
         pieces = [(h, u) for h in range(HALVES) for u in range(Q_TILES)]
-        score_tags = ["bd0_turned", "bd1_turned", "third_score", "last_score"]
+        score_tags = ["first_score", "second_score", "third_score", "last_score"]
         probs = []
         for h, u in pieces:
             slots = slice(h * HALF, (h + 1) * HALF)

@@ -42,6 +42,7 @@ def tile_attend_link_bid_topk_kernel(tc, qT, k_words, k_scales, kb, bd, offs, ou
         bd_win = keep.tile([P, T], F32, name="bd_win")
         q_raw = keep.tile([P, PACK, NQ], F32, name="q_raw")
         nc.sync.dma_start(out=q_raw[:], in_=qT[0].rearrange("(p j) w -> p j w", j=PACK))
+        nc.sync.dma_start(out=bd_win[P - 1 : P, :], in_=bd[0:1, :])
 
         scale_win = keep.tile([P, T], U8, name="scale_win", align_bytes=64)
         nc.vector.memset(scale_win[:].bitcast(I32), 0)
@@ -62,7 +63,6 @@ def tile_attend_link_bid_topk_kernel(tc, qT, k_words, k_scales, kb, bd, offs, ou
             nc.sync.dma_start(
                 out=scale_win[:].bitcast(I32)[r:P:QUADRANT, :], in_=scale_rows[r : D // 32 : SCALE_ROWS, :]
             )
-        nc.sync.dma_start(out=bd_win[P - 1 : P, :], in_=bd[0:1, :])
         word_win = keep.tile([P, T], I32, name="word_win")
         nc.sync.dma_start(out=word_win[:], in_=k_words[0].rearrange("p n t -> p (n t)").bitcast(I32))
 

@@ -113,30 +113,34 @@ def tile_attend_link_bid_topk_kernel(tc, qT, k_words, k_scales, kb, bd, offs, ou
         nc.scalar.copy(out=kb_all[:], in_=kb_wide[:])
         bd_cols.append(to_columns([bd_last[:, 0:P], bd_last[:, P : 2 * P]], "bd1"))
 
-        list_cols = HALF // LIST_ROWS
-        word_g = [keep.tile([P, HALF], U32, name="word_g%d" % h, align_bytes=64) for h in range(HALVES)]
-        for h in range(HALVES):
+        word_g = [keep.tile([P, P], U32, name="word_g%d" % j, align_bytes=64) for j in range(SLOT_TILES)]
+        for j in range(SLOT_TILES):
             nc.vector.tensor_copy(
-                word_g[h][:], word_win[:].bitcast(U32).indirect(offsets[:, h * list_cols : (h + 1) * list_cols])
+                word_g[j][:], word_win[:].bitcast(U32).indirect(offsets[:, j * tile_cols : (j + 1) * tile_cols])
             )
 
         pieces = [(h, u) for h in range(HALVES) for u in range(Q_TILES)]
         score_tags = ["first_score", "second_score", "third_score", "last_score"]
+        scores = {
+            (h, u): psum.tile([P, HALF], F32, name="score%d%d" % (h, u), tag=score_tags[h * Q_TILES + u])
+            for h, u in pieces
+        }
+        for h, u in pieces:
+            for first in range(0, HALF, P):
+                j = (h * HALF + first) // P
+                nc.tensor.matmul_mx(
+                    out=scores[h, u][:, first : first + P],
+                    lhsT=q_codes[u][:].bitcast(FP8X4),
+                    lhsT_scale=q_scales[u][:],
+                    rhs=word_g[j][:].bitcast(FP8X4),
+                    rhs_scale=scale_g[:, j * P : (j + 1) * P],
+                    start=True,
+                    stop=True,
+                )
         probs = []
         for h, u in pieces:
-            slots = slice(h * HALF, (h + 1) * HALF)
-            score = psum.tile([P, HALF], F32, name="score%d%d" % (h, u), tag=score_tags[h * Q_TILES + u])
-            nc.tensor.matmul_mx(
-                out=score[:],
-                lhsT=q_codes[u][:].bitcast(FP8X4),
-                lhsT_scale=q_scales[u][:],
-                rhs=word_g[h][:].bitcast(FP8X4),
-                rhs_scale=scale_g[:, slots],
-                start=True,
-                stop=True,
-            )
             logit = keep.tile([P, HALF], F32, name="logit%d%d" % (h, u))
-            nc.vector.tensor_tensor(logit[:], score[:], kb_all[:, slots], ALU.add)
+            nc.vector.tensor_tensor(logit[:], scores[h, u][:], kb_all[:, h * HALF : (h + 1) * HALF], ALU.add)
             prob = keep.tile([P, HALF], F32, name="prob%d%d" % (h, u))
             nc.scalar.activation(prob[:], logit[:], ACT.Sigmoid)
             probs.append(prob)

@@ -67,12 +67,17 @@ def tile_attend_link_bid_topk_kernel(tc, qT, k_words, k_scales, kb, bd, offs, ou
         nc.sync.dma_start(out=word_win[:], in_=k_words[0].rearrange("p n t -> p (n t)").bitcast(I32))
 
         tile_cols = P // LIST_ROWS
-        kb_first = keep.tile([P, 3 * P], F32, name="kb_first", tag="bias_then_last_bids")
-        nc.scalar.activation(kb_first[:], kb_win[:].indirect(offsets[:, 0 : 3 * tile_cols]), ACT.Copy)
-        kb_last = keep.tile([P, P], F32, name="kb_last")
-        nc.vector.tensor_copy(kb_last[:], kb_win[:].indirect(offsets[:, 3 * tile_cols : 4 * tile_cols]))
-        bd_first = keep.tile([P, HALF], F32, name="bd_first")
-        nc.scalar.activation(bd_first[:], bd_win[:].indirect(offsets[:, 0 : 2 * tile_cols]), ACT.Copy)
+        kb_first = keep.tile([P, P], F32, name="kb_first")
+        nc.scalar.activation(kb_first[:], kb_win[:].indirect(offsets[:, 0:tile_cols]), ACT.Copy)
+        kb_second = keep.tile([P, P], F32, name="kb_second")
+        nc.vector.tensor_copy(kb_second[:], kb_win[:].indirect(offsets[:, tile_cols : 2 * tile_cols]))
+        kb_last = keep.tile([P, HALF], F32, name="kb_last", tag="bias_then_last_bids")
+        nc.scalar.activation(kb_last[:], kb_win[:].indirect(offsets[:, 2 * tile_cols : 4 * tile_cols]), ACT.Copy)
+        bd_first = [keep.tile([P, P], F32, name="bd_first%d" % j) for j in range(2)]
+        for j in range(2):
+            nc.scalar.activation(
+                bd_first[j][:], bd_win[:].indirect(offsets[:, j * tile_cols : (j + 1) * tile_cols]), ACT.Copy
+            )
         q_grp = [keep.tile([P, P, PACK], BF16, name="q_grp%d" % u, align_bytes=64) for u in range(Q_TILES)]
         q_codes = [keep.tile([P, P], U32, name="q_codes%d" % u, align_bytes=64) for u in range(Q_TILES)]
         q_scales = [keep.tile([P, P], U8, name="q_scales%d" % u, align_bytes=64) for u in range(Q_TILES)]
@@ -101,12 +106,12 @@ def tile_attend_link_bid_topk_kernel(tc, qT, k_words, k_scales, kb, bd, offs, ou
                 column = col[:, j : j + 1]
                 nc.tensor.transpose(bank[:, j * P : (j + 1) * P], column.to_broadcast([P, P]), ident[:])
 
-        kb_col = to_columns([kb_first[:, j * P : (j + 1) * P] for j in range(3)] + [kb_last[:]], "kb")
+        kb_col = to_columns([kb_first[:], kb_second[:], kb_last[:, 0:P], kb_last[:, P:HALF]], "kb")
         kb_wide = psum.tile([P, N], F32, name="kb_wide")
         spread(kb_wide, kb_col)
         bd_last = keep.tile([P, HALF], F32, name="bd_last", tag="bias_then_last_bids")
         nc.scalar.activation(bd_last[:], bd_win[:].indirect(offsets[:, 2 * tile_cols : 4 * tile_cols]), ACT.Copy)
-        bd_cols = [to_columns([bd_first[:, 0:P], bd_first[:, P : 2 * P]], "bd0")]
+        bd_cols = [to_columns([bd_first[0][:], bd_first[1][:]], "bd0")]
         bd_wide = [psum.tile([P, HALF], F32, name="bd_wide0", tag="kb_turned")]
         spread(bd_wide[0], bd_cols[0])
         kb_all = keep.tile([P, N], F32, name="kb_all")

@@ -107,7 +107,7 @@ def tile_attend_link_bid_topk_kernel(tc, qT, k_words, k_scales, kb, bd, offs, ou
                 nc.tensor.transpose(bank[:, j * P : (j + 1) * P], column.to_broadcast([P, P]), ident[:])
 
         kb_col = to_columns([kb_first[:], kb_second[:], kb_last[:, 0:P], kb_last[:, P:HALF]], "kb")
-        kb_wide = psum.tile([P, N], F32, name="kb_wide")
+        kb_wide = psum.tile([P, N], F32, name="kb_wide", tag="kb_wide")
         spread(kb_wide, kb_col)
         bd_last = keep.tile([P, HALF], F32, name="bd_last", tag="bias_then_last_bids")
         nc.scalar.activation(bd_last[:], bd_win[:].indirect(offsets[:, 2 * tile_cols : 4 * tile_cols]), ACT.Copy)
@@ -118,42 +118,53 @@ def tile_attend_link_bid_topk_kernel(tc, qT, k_words, k_scales, kb, bd, offs, ou
         nc.scalar.copy(out=kb_all[:], in_=kb_wide[:])
         bd_cols.append(to_columns([bd_last[:, 0:P], bd_last[:, P : 2 * P]], "bd1"))
 
+        bd_half = keep.tile([P, HALF], F32, name="bd_half")
+        nc.scalar.copy(out=bd_half[:], in_=bd_wide[0][:])
+
         word_g = [keep.tile([P, P], U32, name="word_g%d" % j, align_bytes=64) for j in range(SLOT_TILES)]
         for j in range(SLOT_TILES):
             nc.vector.tensor_copy(
                 word_g[j][:], word_win[:].bitcast(U32).indirect(offsets[:, j * tile_cols : (j + 1) * tile_cols])
             )
 
+        units = [(j, u) for j in range(SLOT_TILES) for u in range(Q_TILES)]
+        by_slot = [(0, 1), (1, 1)]
+        by_query = [unit for unit in units if unit not in by_slot]
+        tags = ["unit00", "unit01", "unit10", "unit11", "bd0_turned", "kb_wide", "bd1_turned", "kb_turned"]
+        scores = {}
+        for (j, u), tag in zip(units, tags):
+            scores[j, u] = psum.tile([P, P], F32, name="score%d%d" % (j, u), tag=tag)
+            keys = (word_g[j][:].bitcast(FP8X4), scale_g[:, j * P : (j + 1) * P])
+            queries = (q_codes[u][:].bitcast(FP8X4), q_scales[u][:])
+            held, moving = (keys, queries) if (j, u) in by_slot else (queries, keys)
+            nc.tensor.matmul_mx(
+                out=scores[j, u][:],
+                lhsT=held[0],
+                lhsT_scale=held[1],
+                rhs=moving[0],
+                rhs_scale=moving[1],
+                start=True,
+                stop=True,
+            )
+        slot_probs = []
+        for j, u in by_slot:
+            slot_probs.append(keep.tile([P, P], F32, name="slot_prob%d" % j))
+            nc.scalar.activation(slot_probs[j][:], scores[j, u][:], ACT.Sigmoid, bias=kb_col[:, j : j + 1])
         pieces = [(h, u) for h in range(HALVES) for u in range(Q_TILES)]
-        score_tags = ["first_score", "second_score", "third_score", "last_score"]
-        scores = {
-            (h, u): psum.tile([P, HALF], F32, name="score%d%d" % (h, u), tag=score_tags[h * Q_TILES + u])
-            for h, u in pieces
-        }
-        for h, u in pieces:
-            for first in range(0, HALF, P):
-                j = (h * HALF + first) // P
-                nc.tensor.matmul_mx(
-                    out=scores[h, u][:, first : first + P],
-                    lhsT=q_codes[u][:].bitcast(FP8X4),
-                    lhsT_scale=q_scales[u][:],
-                    rhs=word_g[j][:].bitcast(FP8X4),
-                    rhs_scale=scale_g[:, j * P : (j + 1) * P],
-                    start=True,
-                    stop=True,
-                )
-        probs = []
-        for h, u in pieces:
-            logit = keep.tile([P, HALF], F32, name="logit%d%d" % (h, u))
-            nc.vector.tensor_tensor(logit[:], scores[h, u][:], kb_all[:, h * HALF : (h + 1) * HALF], ALU.add)
-            prob = keep.tile([P, HALF], F32, name="prob%d%d" % (h, u))
-            nc.scalar.activation(prob[:], logit[:], ACT.Sigmoid)
-            probs.append(prob)
+        probs = {(h, u): keep.tile([P, HALF], F32, name="prob%d%d" % (h, u)) for h, u in pieces if (h, u) != (0, 1)}
+        for j, u in by_query:
+            logit = keep.tile([P, P], F32, name="logit%d%d" % (j, u))
+            nc.vector.tensor_tensor(logit[:], scores[j, u][:], kb_all[:, j * P : (j + 1) * P], ALU.add)
+            nc.scalar.activation(probs[j // 2, u][:, (j % 2) * P : (j % 2 + 1) * P], logit[:], ACT.Sigmoid)
 
-        bd_wide.append(psum.tile([P, HALF], F32, name="bd_wide1", tag=score_tags[0]))
+        probs[0, 1] = psum.tile([P, HALF], F32, name="prob_turned", tag="unit00")
+        for j in range(2):
+            nc.tensor.transpose(probs[0, 1][:, j * P : (j + 1) * P], slot_probs[j][:], ident[:])
+        bd_wide.append(psum.tile([P, HALF], F32, name="bd_wide1", tag="unit01"))
         spread(bd_wide[1], bd_cols[1])
-        for (h, u), prob in zip(pieces, probs):
+        bids = [bd_half, bd_wide[1]]
+        for h, u in pieces:
             slots = slice(h * HALF, (h + 1) * HALF)
             res = keep.tile([P, HALF], F32, name="res%d%d" % (h, u))
-            nc.vector.tensor_tensor(res[:], prob[:], bd_wide[h][:], ALU.mult)
+            nc.vector.tensor_tensor(res[:], probs[h, u][:], bids[h][:], ALU.mult)
             nc.sync.dma_start(out=out[0, u * P : (u + 1) * P, slots], in_=res[:])

from contextlib import ExitStack

import concourse.mybir as mybir

F32 = mybir.dt.float32
BF16 = mybir.dt.bfloat16
I32 = mybir.dt.int32
U32 = mybir.dt.uint32
U16 = mybir.dt.uint16
U8 = mybir.dt.uint8
FP8X4 = mybir.dt.float8_e4m3fn_x4
ACT = mybir.ActivationFunctionType
ALU = mybir.AluOpType

P = 128
PACK = 4
T = 2048
N = 512
NQ = 256
D = 512
QUADRANT = 32
SCALE_ROWS = 4
LIST_ROWS = 16
SLOT_TILES = N // P
Q_TILES = NQ // P
HALVES = 2
HALF = N // HALVES

FLOPS = 2 * D * NQ * N


def tile_attend_link_bid_topk_kernel(tc, qT, k_words, k_scales, kb, bd, offs, out):
    nc = tc.nc
    with ExitStack() as ctx:
        keep = ctx.enter_context(tc.tile_pool(name="keep", bufs=1))
        psum = ctx.enter_context(tc.psum_pool(name="psum", bufs=1))

        offsets = keep.tile([P, N // LIST_ROWS], U16, name="offsets")
        nc.sync.dma_start(offsets[:], offs)
        kb_win = keep.tile([P, T], F32, name="kb_win")
        nc.scalar.dma_start(out=kb_win[P - 1 : P, :], in_=kb[0:1, :])
        bd_win = keep.tile([P, T], F32, name="bd_win")
        q_raw = keep.tile([P, PACK, NQ], F32, name="q_raw")
        nc.sync.dma_start(out=q_raw[:], in_=qT[0].rearrange("(p j) w -> p j w", j=PACK))
        nc.sync.dma_start(out=bd_win[P - 1 : P, :], in_=bd[0:1, :])

        scale_win = keep.tile([P, T], U8, name="scale_win", align_bytes=64)
        nc.vector.memset(scale_win[:].bitcast(I32), 0)
        nc.vector.memset(kb_win[0 : P - 1, :].bitcast(I32), 0)
        zeros = keep.tile([P, P], F32, name="zeros")
        nc.vector.memset(zeros[:], 0.0)
        nc.vector.memset(bd_win[0 : P - 1, :].bitcast(I32), 0)
        warm = keep.tile([P, 1], F32, name="warm")
        nc.gpsimd.memset(warm[:], 0.0)
        nc.scalar.activation(warm[:], warm[:], ACT.Sigmoid)
        ident = keep.tile([P, P], F32, name="ident")
        nc.gpsimd.affine_select(
            out=ident[:], in_=zeros[:], compare_op=ALU.not_equal, fill=1.0, base=0, pattern=[[-1, P]], channel_multiplier=1
        )

        scale_rows = k_scales[0].bitcast(I32)
        for r in range(SCALE_ROWS):
            nc.sync.dma_start(
                out=scale_win[:].bitcast(I32)[r:P:QUADRANT, :], in_=scale_rows[r : D // 32 : SCALE_ROWS, :]
            )
        word_win = keep.tile([P, T], I32, name="word_win")
        nc.sync.dma_start(out=word_win[:], in_=k_words[0].rearrange("p n t -> p (n t)").bitcast(I32))

        tile_cols = P // LIST_ROWS
        kb_first = keep.tile([P, P], F32, name="kb_first")
        nc.scalar.activation(kb_first[:], kb_win[:].indirect(offsets[:, 0:tile_cols]), ACT.Copy)
        kb_second = keep.tile([P, P], F32, name="kb_second")
        nc.vector.tensor_copy(kb_second[:], kb_win[:].indirect(offsets[:, tile_cols : 2 * tile_cols]))
        kb_last = keep.tile([P, HALF], F32, name="kb_last", tag="bias_then_last_bids")
        nc.scalar.activation(kb_last[:], kb_win[:].indirect(offsets[:, 2 * tile_cols : 4 * tile_cols]), ACT.Copy)
        bd_first = [keep.tile([P, P], F32, name="bd_first%d" % j) for j in range(2)]
        for j in range(2):
            nc.scalar.activation(
                bd_first[j][:], bd_win[:].indirect(offsets[:, j * tile_cols : (j + 1) * tile_cols]), ACT.Copy
            )
        q_grp = [keep.tile([P, P, PACK], BF16, name="q_grp%d" % u, align_bytes=64) for u in range(Q_TILES)]
        q_codes = [keep.tile([P, P], U32, name="q_codes%d" % u, align_bytes=64) for u in range(Q_TILES)]
        q_scales = [keep.tile([P, P], U8, name="q_scales%d" % u, align_bytes=64) for u in range(Q_TILES)]
        for u in range(Q_TILES):
            nc.vector.tensor_copy(
                out=q_grp[u][:].rearrange("p (c i) t -> p c t i", i=4),
                in_=q_raw[:, :, u * P : (u + 1) * P].rearrange("p t (c i) -> p c t i", i=4),
            )
        for u in range(Q_TILES):
            nc.vector.quantize_mx(
                out=q_codes[u][:].bitcast(FP8X4), scales=q_scales[u][:], in_=q_grp[u][:].rearrange("p w j -> p (w j)")
            )
        scale_g = keep.tile([P, N], U8, name="scale_g", align_bytes=64)
        nc.vector.tensor_copy(scale_g[:], scale_win[:].indirect(offsets[:]))

        def to_columns(tiles, name):
            turned = psum.tile([P, len(tiles), P], F32, name=name + "_turned", tag=name + "_turned")
            for j in range(len(tiles)):
                nc.tensor.transpose(turned[:, j, :], tiles[j], ident[:])
            col = keep.tile([P, len(tiles)], F32, name=name + "_col")
            nc.scalar.copy(out=col[:], in_=turned[:, :, P - 1])
            return col

        def spread(bank, col):
            for j in range(bank.shape[1] // P):
                column = col[:, j : j + 1]
                nc.tensor.transpose(bank[:, j * P : (j + 1) * P], column.to_broadcast([P, P]), ident[:])

        kb_col = to_columns([kb_first[:], kb_second[:], kb_last[:, 0:P], kb_last[:, P:HALF]], "kb")
        kb_wide = psum.tile([P, N], F32, name="kb_wide", tag="kb_wide")
        spread(kb_wide, kb_col)
        bd_last = keep.tile([P, HALF], F32, name="bd_last", tag="bias_then_last_bids")
        nc.scalar.activation(bd_last[:], bd_win[:].indirect(offsets[:, 2 * tile_cols : 4 * tile_cols]), ACT.Copy)
        bd_cols = [to_columns([bd_first[0][:], bd_first[1][:]], "bd0")]
        bd_wide = [psum.tile([P, HALF], F32, name="bd_wide0", tag="kb_turned")]
        spread(bd_wide[0], bd_cols[0])
        kb_all = keep.tile([P, N], F32, name="kb_all")
        nc.scalar.copy(out=kb_all[:], in_=kb_wide[:])
        bd_cols.append(to_columns([bd_last[:, 0:P], bd_last[:, P : 2 * P]], "bd1"))

        bd_half = keep.tile([P, HALF], F32, name="bd_half")
        nc.scalar.copy(out=bd_half[:], in_=bd_wide[0][:])

        word_g = [keep.tile([P, P], U32, name="word_g%d" % j, align_bytes=64) for j in range(SLOT_TILES)]
        for j in range(SLOT_TILES):
            nc.vector.tensor_copy(
                word_g[j][:], word_win[:].bitcast(U32).indirect(offsets[:, j * tile_cols : (j + 1) * tile_cols])
            )

        units = [(j, u) for j in range(SLOT_TILES) for u in range(Q_TILES)]
        by_slot = [(0, 1), (1, 1)]
        by_query = [unit for unit in units if unit not in by_slot]
        tags = ["unit00", "unit01", "unit10", "unit11", "bd0_turned", "kb_wide", "bd1_turned", "kb_turned"]
        scores = {}
        for (j, u), tag in zip(units, tags):
            scores[j, u] = psum.tile([P, P], F32, name="score%d%d" % (j, u), tag=tag)
            keys = (word_g[j][:].bitcast(FP8X4), scale_g[:, j * P : (j + 1) * P])
            queries = (q_codes[u][:].bitcast(FP8X4), q_scales[u][:])
            held, moving = (keys, queries) if (j, u) in by_slot else (queries, keys)
            nc.tensor.matmul_mx(
                out=scores[j, u][:],
                lhsT=held[0],
                lhsT_scale=held[1],
                rhs=moving[0],
                rhs_scale=moving[1],
                start=True,
                stop=True,
            )
        slot_probs = []
        for j, u in by_slot:
            slot_probs.append(keep.tile([P, P], F32, name="slot_prob%d" % j))
            nc.scalar.activation(slot_probs[j][:], scores[j, u][:], ACT.Sigmoid, bias=kb_col[:, j : j + 1])
        pieces = [(h, u) for h in range(HALVES) for u in range(Q_TILES)]
        probs = {(h, u): keep.tile([P, HALF], F32, name="prob%d%d" % (h, u)) for h, u in pieces if (h, u) != (0, 1)}
        for j, u in by_query:
            logit = keep.tile([P, P], F32, name="logit%d%d" % (j, u))
            nc.vector.tensor_tensor(logit[:], scores[j, u][:], kb_all[:, j * P : (j + 1) * P], ALU.add)
            nc.scalar.activation(probs[j // 2, u][:, (j % 2) * P : (j % 2 + 1) * P], logit[:], ACT.Sigmoid)

        probs[0, 1] = psum.tile([P, HALF], F32, name="prob_turned", tag="unit00")
        for j in range(2):
            nc.tensor.transpose(probs[0, 1][:, j * P : (j + 1) * P], slot_probs[j][:], ident[:])
        bd_wide.append(psum.tile([P, HALF], F32, name="bd_wide1", tag="unit01"))
        spread(bd_wide[1], bd_cols[1])
        bids = [bd_half, bd_wide[1]]
        for h, u in pieces:
            slots = slice(h * HALF, (h + 1) * HALF)
            res = keep.tile([P, HALF], F32, name="res%d%d" % (h, u))
            nc.vector.tensor_tensor(res[:], probs[h, u][:], bids[h][:], ALU.mult)
            nc.sync.dma_start(out=out[0, u * P : (u + 1) * P, slots], in_=res[:])
